import numpy as np
import ml_dtypes


def mxq(x, axis, fmt="e4m3"):
    dtype, down = {"e4m3": (ml_dtypes.float8_e4m3fn, 7), "e5m2": (ml_dtypes.float8_e5m2, 14)}[fmt]
    v = np.moveaxis(np.asarray(x, np.float32).astype(ml_dtypes.bfloat16).astype(np.float64), axis, -1)
    blocks = v.reshape(v.shape[:-1] + (-1, 32))
    amax = np.abs(blocks).max(-1, keepdims=True)
    byte = np.maximum(np.where(amax > 0, np.frexp(amax)[1] - 1 + 127, 0) - down, 1)
    scale = np.exp2(byte - 127.0)
    codes = (blocks / scale).astype(np.float32).astype(dtype).astype(np.float64)
    return np.moveaxis((codes * scale).reshape(v.shape), -1, axis)


WIDE = False


def mx_kscale(k):
    if not WIDE:
        return np.ones(k)
    levels = np.array([30, -30])
    if k % 512:
        return np.exp2(np.random.permutation(np.resize(levels, k // 32))).repeat(32)
    a = np.empty((k // 512, 16))
    for p in range(k // 512):
        a[p, :8] = np.random.permutation(np.resize(levels, 8))
        for g in range(8):
            far = levels[np.abs(levels - a[p, g]) >= 10]
            a[p, g + 8] = far[np.random.randint(len(far))]
    return np.exp2(a.ravel()).repeat(32)


def f64(x):
    return np.asarray(x).astype(np.float64)


def striped(idx):
    return np.tile(np.asarray(idx).reshape(-1, 16).T, (8, 1)).astype(np.uint16)


def unstriped(offs):
    return offs[:16].T.reshape(-1).astype(np.int64)


E2M1 = np.array([0.0, 0.5, 1.0, 1.5, 2.0, 3.0, 4.0, 6.0, -0.0, -0.5, -1.0, -1.5, -2.0, -3.0, -4.0, -6.0])


def pack_weight(w, fmt):
    k, n = w.shape
    w = f64(np.asarray(w, np.float32).astype(ml_dtypes.bfloat16)).reshape(k // 32, 32, n)
    amax = np.abs(w).max(1)
    if fmt in ("e4m3", "e5m2"):
        byte = np.frexp(amax)[1] - 1 + 127 - (7 if fmt == "e4m3" else 14)
    else:
        mant, ex = np.frexp(amax / 6.0)
        byte = np.where(mant > 0.5, ex, ex - 1) + 127
    byte = np.clip(np.where(amax > 0, byte, 1), 1, 254)
    scaled = (w * np.exp2(127.0 - byte)[:, None, :]).reshape(k, n).astype(np.float32)
    by_word = np.ascontiguousarray(scaled.reshape(k // 512, 128, 4, n).transpose(0, 1, 3, 2))
    if fmt in ("e4m3", "e5m2"):
        words = by_word.astype(ml_dtypes.float8_e4m3fn if fmt == "e4m3" else ml_dtypes.float8_e5m2).view(np.uint8)
    else:
        c = by_word.astype(ml_dtypes.float4_e2m1fn).view(np.uint8) & 0xF
        words = (c[..., 0::2] | (c[..., 1::2] << 4)).reshape(k // 512, 128, 2 * n)
    return np.ascontiguousarray(words), np.ascontiguousarray(byte.astype(np.uint8).reshape(k // 512, 16, n))


def unpack_weight(words, scales, fmt):
    g, _, n = scales.shape
    words = np.ascontiguousarray(words).reshape(g, 128, n, -1)
    if fmt in ("e4m3", "e5m2"):
        vals = words.view(ml_dtypes.float8_e4m3fn if fmt == "e4m3" else ml_dtypes.float8_e5m2).astype(np.float64)
    else:
        nib = np.empty((g, 128, n, 4), np.uint8)
        nib[..., 0::2] = words & 0xF
        nib[..., 1::2] = words >> 4
        vals = E2M1[nib]
    vals = vals * np.repeat(np.exp2(scales.astype(np.float64) - 127.0), 8, axis=1)[..., None]
    return vals.transpose(0, 1, 3, 2).reshape(g * 512, n)


K, T, I, J, N, Z, S, V, O, E = 512, 1024, 512, 256, 256, 1024, 1024, 1024, 128, 1024


def setup_inputs():
    n = np.random.standard_normal
    idx = np.random.permutation(T)[:I]
    idx2 = np.random.permutation(Z)[:J]
    idx3 = np.random.permutation(V)[:J]
    idx4 = np.random.permutation(J)[:O]
    idx5 = np.random.permutation(J)[:O]
    idx6 = np.random.permutation(S)[:N]
    idx7 = np.random.permutation(E)[:O]
    fk = mx_kscale(K)
    fi = mx_kscale(I)
    ti = np.ones(T)
    ti[idx] = fi
    xkp = pack_weight(n((K, T)) * 0.3 * fk[:, None] * ti, "e5m2")
    xqp = pack_weight(n((K, Z)) * 0.3 / fk[:, None], "e2m1")
    xrp = pack_weight(n((K, V)) * 0.3 / fk[:, None], "e5m2")
    vsp = pack_weight(n((I, S)) / fi[:, None], "e5m2")
    return {
        "xk_words": xkp[0],
        "xk_scales": xkp[1],
        "xq_words": xqp[0],
        "xq_scales": xqp[1],
        "xr_words": xrp[0],
        "xr_scales": xrp[1],
        "vs_words": vsp[0],
        "vs_scales": vsp[1],
        "offs": striped(idx),
        "offs2": striped(idx2),
        "offs3": striped(idx3),
        "offs4": striped(idx4),
        "offs5": striped(idx5),
        "offs6": striped(idx6),
        "offs7": striped(idx7),
    }


def reference(xk_words, xk_scales, xq_words, xq_scales, xr_words, xr_scales, vs_words, vs_scales, offs, offs2, offs3, offs4, offs5, offs6, offs7):
    idx = unstriped(offs)
    idx2 = unstriped(offs2)
    idx3 = unstriped(offs3)
    idx4 = unstriped(offs4)
    idx5 = unstriped(offs5)
    idx6 = unstriped(offs6)
    idx7 = unstriped(offs7)
    xku = unpack_weight(xk_words, xk_scales, "e5m2")
    xqu = unpack_weight(xq_words, xq_scales, "e2m1")
    xru = unpack_weight(xr_words, xr_scales, "e5m2")
    vsu = unpack_weight(vs_words, vs_scales, "e5m2")
    xkidxg = xku[:, idx]
    xqidx2g = xqu[:, idx2]
    s1 = xkidxg.T @ xqidx2g
    xridx3g = xru[:, idx3]
    s2 = xkidxg.T @ xridx3g
    hid = np.maximum(s1[:, idx4] - s2[:, idx5], 0.0)
    vsidx6g = vsu[:, idx6]
    hidq = mxq(hid, 0, "e4m3")
    p = vsidx6g.T @ hidq
    y = np.zeros((N, E))
    y[:, idx7] = p
    return y

@@ -1,0 +1,142 @@
+from contextlib import ExitStack
+
+import concourse.mybir as mybir
+
+K, T, I, J, N, O, E = 512, 1024, 512, 256, 256, 128, 1024
+FLOPS = 2 * K * I * J * 2 + 2 * I * N * O
+
+F32 = mybir.dt.float32
+BF16 = mybir.dt.bfloat16
+I32 = mybir.dt.int32
+U32 = mybir.dt.uint32
+U16 = mybir.dt.uint16
+U8 = mybir.dt.uint8
+E5M2 = mybir.dt.float8_e5m2_x4
+E4M3 = mybir.dt.float8_e4m3fn_x4
+E2M1 = mybir.dt.float4_e2m1fn_x4
+ALU = mybir.AluOpType
+ACT = mybir.ActivationFunctionType
+
+P = 128
+PACK = 4
+QUADS = 4
+
+
+def tile_list_contest_rivals_looked_scattered_kernel(
+    tc, xk_words, xk_scales, xq_words, xq_scales, xr_words, xr_scales, vs_words, vs_scales,
+    offs, offs2, offs3, offs4, offs5, offs6, offs7, out,
+):
+    nc = tc.nc
+    with ExitStack() as ctx:
+        pool = ctx.enter_context(tc.tile_pool(name="pool", bufs=1))
+        psum = ctx.enter_context(tc.psum_pool(name="psum", bufs=1))
+
+        def load_list(name, source):
+            tile = pool.tile(list(source.shape), U16, name=name)
+            nc.sync.dma_start(tile[:], source)
+            return tile
+
+        def load_words(name, source, dtype, queue):
+            tile = pool.tile([P, T], dtype, name=name, align_bytes=64)
+            queue.dma_start(tile[:].bitcast(I32), source.bitcast(I32))
+            return tile
+
+        def zeroed_plane(name):
+            tile = pool.tile([P, T], U8, name=name, align_bytes=64)
+            nc.vector.memset(tile[:].bitcast(I32), 0)
+            return tile
+
+        def load_scales(tile, source, queue):
+            for q in range(QUADS):
+                queue.dma_start(tile[32 * q : 32 * q + 4, :].bitcast(I32), source[0, 4 * q : 4 * q + 4, :].bitcast(I32))
+
+        def gather(name, window, offsets, count, dtype):
+            tile = pool.tile([P, count], dtype, name=name, align_bytes=64)
+            nc.vector.tensor_copy(tile[:], window[:].indirect(offsets[:]))
+            return tile
+
+        def gather_dealt(name, window, offsets, dtype):
+            tile = pool.tile([P, PACK, P], dtype, name=name, align_bytes=64)
+            nc.vector.tensor_copy(tile[:].rearrange("p t q -> p q t"), window[:].indirect(offsets[:]))
+            return tile
+
+        k_plane = zeroed_plane("k_plane")
+        q_plane = zeroed_plane("q_plane")
+        r_plane = zeroed_plane("r_plane")
+        v_plane = zeroed_plane("v_plane")
+        pages = [pool.tile([P, E], F32, name=f"page{h}") for h in range(2)]
+        for page in pages:
+            nc.vector.memset(page[:], 0.0)
+
+        k_list = load_list("k_list", offs)
+        q_list = load_list("q_list", offs2)
+        q_table = load_words("q_table", xq_words[0], U16, nc.sync)
+        load_scales(k_plane, xk_scales, nc.scalar)
+        k_table = load_words("k_table", xk_words[0].rearrange("p c r -> p (c r)"), U32, nc.sync)
+        load_scales(q_plane, xq_scales, nc.sync)
+        load_scales(r_plane, xr_scales, nc.gpsimd)
+        load_scales(v_plane, vs_scales, nc.gpsimd)
+        r_list = load_list("r_list", offs3)
+        r_table = load_words("r_table", xr_words[0].rearrange("p c r -> p (c r)"), U32, nc.sync)
+        v_list = load_list("v_list", offs6)
+        v_table = load_words("v_table", vs_words[0].rearrange("p c r -> p (c r)"), U32, nc.sync)
+        first_list = load_list("first_list", offs4)
+        second_list = load_list("second_list", offs5)
+        page_list = load_list("page_list", offs7)
+
+        k_bytes = gather_dealt("k_bytes", k_plane, k_list, U8)
+        q_words = gather("q_words", q_table, q_list, J, U16)
+        k_words = gather_dealt("k_words", k_table, k_list, U32)
+        q_bytes = gather("q_bytes", q_plane, q_list, J, U8)
+        r_words = gather("r_words", r_table, r_list, J, U32)
+        r_bytes = gather("r_bytes", r_plane, r_list, J, U8)
+        v_words = gather("v_words", v_table, v_list, N, U32)
+        v_bytes = gather("v_bytes", v_plane, v_list, N, U8)
+
+        def scores(tag, t, words, scale_bytes):
+            bank = psum.tile([P, J], F32, name=f"{tag}{t}")
+            nc.tensor.matmul_mx(
+                bank[:], lhsT=k_words[:, t, :].bitcast(E5M2), lhsT_scale=k_bytes[:, t, :],
+                rhs=words, rhs_scale=scale_bytes[:], start=True, stop=True,
+            )
+            return bank
+
+        s1_banks = [scores("s1_bank", t, q_words[:].bitcast(E2M1), q_bytes) for t in range(PACK)]
+        s2_banks = [scores("s2_bank", t, r_words[:].bitcast(E5M2), r_bytes) for t in range(PACK)]
+
+        s1 = [pool.tile([P, J], F32, name=f"s1_{t}") for t in range(PACK)]
+        s2 = [pool.tile([P, J], F32, name=f"s2_{t}") for t in range(PACK)]
+        first = [pool.tile([P, O], F32, name=f"first{t}") for t in range(PACK)]
+        below = pool.tile([P, PACK, O], F32)
+        for t in range(PACK):
+            nc.scalar.copy(s1[t][:], s1_banks[t][:])
+        for t in range(PACK):
+            if t == PACK - 1:
+                nc.vector.tensor_copy(s2[t][:], s2_banks[t][:])
+            else:
+                nc.scalar.copy(s2[t][:], s2_banks[t][:])
+            nc.scalar.activation(first[t][:], s1[t][:].indirect(first_list[:]), ACT.Copy)
+            nc.vector.tensor_tensor(below[:, t, :], s2[t][:].indirect(second_list[:]), first[t][:], ALU.subtract)
+
+        hid = pool.tile([P, O, PACK], BF16, align_bytes=64)
+        nc.vector.tensor_scalar(hid[:], below[:].rearrange("p t o -> p o t"), -1.0, 0.0, ALU.mult, ALU.max)
+        hid_words = pool.tile([P, O], U32, align_bytes=64)
+        hid_bytes = pool.tile([P, O], U8, align_bytes=64)
+        nc.vector.quantize_mx(hid_words[:].bitcast(E4M3), hid_bytes[:], hid[:].rearrange("p o t -> p (o t)"))
+
+        for h in range(2):
+            rows = slice(h * P, (h + 1) * P)
+            bank = psum.tile([P, O], F32, name=f"p_bank{h}", tag=f"s1_bank{h}")
+            nc.tensor.matmul_mx(
+                bank[:], lhsT=v_words[:, rows].bitcast(E5M2), lhsT_scale=v_bytes[:, rows],
+                rhs=hid_words[:].bitcast(E4M3), rhs_scale=hid_bytes[:], start=True, stop=True,
+            )
+            product = pool.tile([P, O], F32, name=f"product{h}")
+            if h == 0:
+                nc.scalar.copy(product[:], bank[:])
+                nc.scalar.activation(pages[h][:].indirect(page_list[:]), product[:], ACT.Copy)
+                nc.scalar.dma_start(out[rows, :], pages[h][:])
+            else:
+                nc.vector.tensor_copy(product[:], bank[:])
+                nc.vector.tensor_copy(pages[h][:].indirect(page_list[:]), product[:])
+                nc.sync.dma_start(out[rows, :], pages[h][:])

@@ -41,9 +41,9 @@ def tile_list_contest_rivals_looked_scattered_kernel(
             queue.dma_start(tile[:].bitcast(I32), source.bitcast(I32))
             return tile
 
-        def zeroed_plane(name):
+        def zeroed_plane(name, engine):
             tile = pool.tile([P, T], U8, name=name, align_bytes=64)
-            nc.vector.memset(tile[:].bitcast(I32), 0)
+            engine.memset(tile[:].bitcast(I32), 0)
             return tile
 
         def load_scales(tile, source, queue):
@@ -60,27 +60,32 @@ def tile_list_contest_rivals_looked_scattered_kernel(
             nc.vector.tensor_copy(tile[:].rearrange("p t q -> p q t"), window[:].indirect(offsets[:]))
             return tile
 
-        k_plane = zeroed_plane("k_plane")
-        q_plane = zeroed_plane("q_plane")
-        r_plane = zeroed_plane("r_plane")
-        v_plane = zeroed_plane("v_plane")
+        def load_scales_repeated(name, source, queues):
+            tile = pool.tile([P, T], U8, name=name, align_bytes=64)
+            for q in range(QUADS):
+                rows = source[0, 4 * q : 4 * q + 4, :].bitcast(I32)
+                queues[q % len(queues)].dma_start(tile[32 * q : 32 * (q + 1), :].bitcast(I32), rows.unsqueeze(0).broadcast_to([8, 4, T // 4]))
+            return tile
+
+        v_plane = zeroed_plane("v_plane", nc.gpsimd)
+        load_scales(v_plane, vs_scales, nc.gpsimd)
+        r_plane = zeroed_plane("r_plane", nc.vector)
         pages = [pool.tile([P, E], F32, name=f"page{h}") for h in range(2)]
         for page in pages:
             nc.vector.memset(page[:], 0.0)
 
         k_list = load_list("k_list", offs)
+        k_plane = load_scales_repeated("k_plane", xk_scales, [nc.scalar, nc.sync])
         q_list = load_list("q_list", offs2)
-        q_table = load_words("q_table", xq_words[0], U16, nc.sync)
-        load_scales(k_plane, xk_scales, nc.scalar)
+        q_table = load_words("q_table", xq_words[0], U16, nc.scalar)
         k_table = load_words("k_table", xk_words[0].rearrange("p c r -> p (c r)"), U32, nc.sync)
-        load_scales(q_plane, xq_scales, nc.sync)
-        load_scales(r_plane, xr_scales, nc.gpsimd)
-        load_scales(v_plane, vs_scales, nc.gpsimd)
+        q_plane = load_scales_repeated("q_plane", xq_scales, [nc.sync])
         r_list = load_list("r_list", offs3)
         r_table = load_words("r_table", xr_words[0].rearrange("p c r -> p (c r)"), U32, nc.sync)
+        load_scales(r_plane, xr_scales, nc.sync)
+        first_list = load_list("first_list", offs4)
         v_list = load_list("v_list", offs6)
         v_table = load_words("v_table", vs_words[0].rearrange("p c r -> p (c r)"), U32, nc.sync)
-        first_list = load_list("first_list", offs4)
         second_list = load_list("second_list", offs5)
         page_list = load_list("page_list", offs7)
 
@@ -105,9 +110,11 @@ def tile_list_contest_rivals_looked_scattered_kernel(
         s2_banks = [scores("s2_bank", t, r_words[:].bitcast(E5M2), r_bytes) for t in range(PACK)]
 
         s1 = [pool.tile([P, J], F32, name=f"s1_{t}") for t in range(PACK)]
-        s2 = [pool.tile([P, J], F32, name=f"s2_{t}") for t in range(PACK)]
+        s2 = [pool.tile([P, J], F32, name=f"s2_{t}") for t in range(PACK - 1)]
+        s2.append(pool.tile([P, J], F32, name="s2_last", tag="v_table", align_bytes=64))
         first = [pool.tile([P, O], F32, name=f"first{t}") for t in range(PACK)]
-        below = pool.tile([P, PACK, O], F32)
+        below = pool.tile([P, PACK, O], F32, tag="v_plane", align_bytes=64)
+        halves = [(slice(0, 4), slice(0, O // 2)), (slice(4, 8), slice(O // 2, O))]
         for t in range(PACK):
             nc.scalar.copy(s1[t][:], s1_banks[t][:])
         for t in range(PACK):
@@ -116,13 +123,16 @@ def tile_list_contest_rivals_looked_scattered_kernel(
             else:
                 nc.scalar.copy(s2[t][:], s2_banks[t][:])
             nc.scalar.activation(first[t][:], s1[t][:].indirect(first_list[:]), ACT.Copy)
-            nc.vector.tensor_tensor(below[:, t, :], s2[t][:].indirect(second_list[:]), first[t][:], ALU.subtract)
+            for entries, cols in ([(slice(0, 8), slice(0, O))] if t < PACK - 1 else halves):
+                nc.vector.tensor_tensor(below[:, t, cols], s2[t][:].indirect(second_list[:, entries]), first[t][:, cols], ALU.subtract)
 
         hid = pool.tile([P, O, PACK], BF16, align_bytes=64)
-        nc.vector.tensor_scalar(hid[:], below[:].rearrange("p t o -> p o t"), -1.0, 0.0, ALU.mult, ALU.max)
+        for entries, cols in halves:
+            nc.vector.tensor_scalar(hid[:, cols, :], below[:, :, cols].rearrange("p t o -> p o t"), -1.0, 0.0, ALU.mult, ALU.max)
         hid_words = pool.tile([P, O], U32, align_bytes=64)
         hid_bytes = pool.tile([P, O], U8, align_bytes=64)
-        nc.vector.quantize_mx(hid_words[:].bitcast(E4M3), hid_bytes[:], hid[:].rearrange("p o t -> p (o t)"))
+        for entries, cols in halves:
+            nc.vector.quantize_mx(hid_words[:, cols].bitcast(E4M3), hid_bytes[:, cols], hid[:, cols, :].rearrange("p o t -> p (o t)"))
 
         for h in range(2):
             rows = slice(h * P, (h + 1) * P)

@@ -69,6 +69,7 @@ def tile_list_contest_rivals_looked_scattered_kernel(
 
         v_plane = zeroed_plane("v_plane", nc.gpsimd)
         load_scales(v_plane, vs_scales, nc.gpsimd)
+        q_plane = zeroed_plane("q_plane", nc.vector)
         r_plane = zeroed_plane("r_plane", nc.vector)
         pages = [pool.tile([P, E], F32, name=f"page{h}") for h in range(2)]
         for page in pages:
@@ -79,7 +80,7 @@ def tile_list_contest_rivals_looked_scattered_kernel(
         q_list = load_list("q_list", offs2)
         q_table = load_words("q_table", xq_words[0], U16, nc.scalar)
         k_table = load_words("k_table", xk_words[0].rearrange("p c r -> p (c r)"), U32, nc.sync)
-        q_plane = load_scales_repeated("q_plane", xq_scales, [nc.sync])
+        load_scales(q_plane, xq_scales, nc.sync)
         r_list = load_list("r_list", offs3)
         r_table = load_words("r_table", xr_words[0].rearrange("p c r -> p (c r)"), U32, nc.sync)
         load_scales(r_plane, xr_scales, nc.sync)

from contextlib import ExitStack

import concourse.mybir as mybir

K, T, I, J, N, O, E = 512, 1024, 512, 256, 256, 128, 1024
FLOPS = 2 * K * I * J * 2 + 2 * I * N * O

F32 = mybir.dt.float32
BF16 = mybir.dt.bfloat16
I32 = mybir.dt.int32
U32 = mybir.dt.uint32
U16 = mybir.dt.uint16
U8 = mybir.dt.uint8
E5M2 = mybir.dt.float8_e5m2_x4
E4M3 = mybir.dt.float8_e4m3fn_x4
E2M1 = mybir.dt.float4_e2m1fn_x4
ALU = mybir.AluOpType
ACT = mybir.ActivationFunctionType

P = 128
PACK = 4
QUADS = 4


def tile_list_contest_rivals_looked_scattered_kernel(
    tc, xk_words, xk_scales, xq_words, xq_scales, xr_words, xr_scales, vs_words, vs_scales,
    offs, offs2, offs3, offs4, offs5, offs6, offs7, out,
):
    nc = tc.nc
    with ExitStack() as ctx:
        pool = ctx.enter_context(tc.tile_pool(name="pool", bufs=1))
        psum = ctx.enter_context(tc.psum_pool(name="psum", bufs=1))

        def load_list(name, source):
            tile = pool.tile(list(source.shape), U16, name=name)
            nc.sync.dma_start(tile[:], source)
            return tile

        def load_words(name, source, dtype, queue):
            tile = pool.tile([P, T], dtype, name=name, align_bytes=64)
            queue.dma_start(tile[:].bitcast(I32), source.bitcast(I32))
            return tile

        def zeroed_plane(name, engine):
            tile = pool.tile([P, T], U8, name=name, align_bytes=64)
            engine.memset(tile[:].bitcast(I32), 0)
            return tile

        def load_scales(tile, source, queue):
            for q in range(QUADS):
                queue.dma_start(tile[32 * q : 32 * q + 4, :].bitcast(I32), source[0, 4 * q : 4 * q + 4, :].bitcast(I32))

        def gather(name, window, offsets, count, dtype):
            tile = pool.tile([P, count], dtype, name=name, align_bytes=64)
            nc.vector.tensor_copy(tile[:], window[:].indirect(offsets[:]))
            return tile

        def gather_dealt(name, window, offsets, dtype):
            tile = pool.tile([P, PACK, P], dtype, name=name, align_bytes=64)
            nc.vector.tensor_copy(tile[:].rearrange("p t q -> p q t"), window[:].indirect(offsets[:]))
            return tile

        def load_scales_repeated(name, source, queues):
            tile = pool.tile([P, T], U8, name=name, align_bytes=64)
            for q in range(QUADS):
                rows = source[0, 4 * q : 4 * q + 4, :].bitcast(I32)
                queues[q % len(queues)].dma_start(tile[32 * q : 32 * (q + 1), :].bitcast(I32), rows.unsqueeze(0).broadcast_to([8, 4, T // 4]))
            return tile

        v_plane = zeroed_plane("v_plane", nc.gpsimd)
        load_scales(v_plane, vs_scales, nc.gpsimd)
        q_plane = zeroed_plane("q_plane", nc.vector)
        r_plane = zeroed_plane("r_plane", nc.vector)
        pages = [pool.tile([P, E], F32, name=f"page{h}") for h in range(2)]
        for page in pages:
            nc.vector.memset(page[:], 0.0)

        k_list = load_list("k_list", offs)
        k_plane = load_scales_repeated("k_plane", xk_scales, [nc.scalar, nc.sync])
        q_list = load_list("q_list", offs2)
        q_table = load_words("q_table", xq_words[0], U16, nc.scalar)
        k_table = load_words("k_table", xk_words[0].rearrange("p c r -> p (c r)"), U32, nc.sync)
        load_scales(q_plane, xq_scales, nc.sync)
        r_list = load_list("r_list", offs3)
        r_table = load_words("r_table", xr_words[0].rearrange("p c r -> p (c r)"), U32, nc.sync)
        load_scales(r_plane, xr_scales, nc.sync)
        first_list = load_list("first_list", offs4)
        v_list = load_list("v_list", offs6)
        v_table = load_words("v_table", vs_words[0].rearrange("p c r -> p (c r)"), U32, nc.sync)
        second_list = load_list("second_list", offs5)
        page_list = load_list("page_list", offs7)

        k_bytes = gather_dealt("k_bytes", k_plane, k_list, U8)
        q_words = gather("q_words", q_table, q_list, J, U16)
        k_words = gather_dealt("k_words", k_table, k_list, U32)
        q_bytes = gather("q_bytes", q_plane, q_list, J, U8)
        r_words = gather("r_words", r_table, r_list, J, U32)
        r_bytes = gather("r_bytes", r_plane, r_list, J, U8)
        v_words = gather("v_words", v_table, v_list, N, U32)
        v_bytes = gather("v_bytes", v_plane, v_list, N, U8)

        def scores(tag, t, words, scale_bytes):
            bank = psum.tile([P, J], F32, name=f"{tag}{t}")
            nc.tensor.matmul_mx(
                bank[:], lhsT=k_words[:, t, :].bitcast(E5M2), lhsT_scale=k_bytes[:, t, :],
                rhs=words, rhs_scale=scale_bytes[:], start=True, stop=True,
            )
            return bank

        s1_banks = [scores("s1_bank", t, q_words[:].bitcast(E2M1), q_bytes) for t in range(PACK)]
        s2_banks = [scores("s2_bank", t, r_words[:].bitcast(E5M2), r_bytes) for t in range(PACK)]

        s1 = [pool.tile([P, J], F32, name=f"s1_{t}") for t in range(PACK)]
        s2 = [pool.tile([P, J], F32, name=f"s2_{t}") for t in range(PACK - 1)]
        s2.append(pool.tile([P, J], F32, name="s2_last", tag="v_table", align_bytes=64))
        first = [pool.tile([P, O], F32, name=f"first{t}") for t in range(PACK)]
        below = pool.tile([P, PACK, O], F32, tag="v_plane", align_bytes=64)
        halves = [(slice(0, 4), slice(0, O // 2)), (slice(4, 8), slice(O // 2, O))]
        for t in range(PACK):
            nc.scalar.copy(s1[t][:], s1_banks[t][:])
        for t in range(PACK):
            if t == PACK - 1:
                nc.vector.tensor_copy(s2[t][:], s2_banks[t][:])
            else:
                nc.scalar.copy(s2[t][:], s2_banks[t][:])
            nc.scalar.activation(first[t][:], s1[t][:].indirect(first_list[:]), ACT.Copy)
            for entries, cols in ([(slice(0, 8), slice(0, O))] if t < PACK - 1 else halves):
                nc.vector.tensor_tensor(below[:, t, cols], s2[t][:].indirect(second_list[:, entries]), first[t][:, cols], ALU.subtract)

        hid = pool.tile([P, O, PACK], BF16, align_bytes=64)
        for entries, cols in halves:
            nc.vector.tensor_scalar(hid[:, cols, :], below[:, :, cols].rearrange("p t o -> p o t"), -1.0, 0.0, ALU.mult, ALU.max)
        hid_words = pool.tile([P, O], U32, align_bytes=64)
        hid_bytes = pool.tile([P, O], U8, align_bytes=64)
        for entries, cols in halves:
            nc.vector.quantize_mx(hid_words[:, cols].bitcast(E4M3), hid_bytes[:, cols], hid[:, cols, :].rearrange("p o t -> p (o t)"))

        for h in range(2):
            rows = slice(h * P, (h + 1) * P)
            bank = psum.tile([P, O], F32, name=f"p_bank{h}", tag=f"s1_bank{h}")
            nc.tensor.matmul_mx(
                bank[:], lhsT=v_words[:, rows].bitcast(E5M2), lhsT_scale=v_bytes[:, rows],
                rhs=hid_words[:].bitcast(E4M3), rhs_scale=hid_bytes[:], start=True, stop=True,
            )
            product = pool.tile([P, O], F32, name=f"product{h}")
            if h == 0:
                nc.scalar.copy(product[:], bank[:])
                nc.scalar.activation(pages[h][:].indirect(page_list[:]), product[:], ACT.Copy)
                nc.scalar.dma_start(out[rows, :], pages[h][:])
            else:
                nc.vector.tensor_copy(product[:], bank[:])
                nc.vector.tensor_copy(pages[h][:].indirect(page_list[:]), product[:])
                nc.sync.dma_start(out[rows, :], pages[h][:])
